import numpy as np
import ml_dtypes


def mxq(x, axis, fmt="e4m3"):
    dtype, down = {"e4m3": (ml_dtypes.float8_e4m3fn, 7), "e5m2": (ml_dtypes.float8_e5m2, 14)}[fmt]
    v = np.moveaxis(np.asarray(x, np.float32).astype(ml_dtypes.bfloat16).astype(np.float64), axis, -1)
    blocks = v.reshape(v.shape[:-1] + (-1, 32))
    amax = np.abs(blocks).max(-1, keepdims=True)
    byte = np.maximum(np.where(amax > 0, np.frexp(amax)[1] - 1 + 127, 0) - down, 1)
    scale = np.exp2(byte - 127.0)
    codes = (blocks / scale).astype(np.float32).astype(dtype).astype(np.float64)
    return np.moveaxis((codes * scale).reshape(v.shape), -1, axis)


WIDE = False


def mx_kscale(k):
    if not WIDE:
        return np.ones(k)
    levels = np.array([30, -30])
    if k % 512:
        return np.exp2(np.random.permutation(np.resize(levels, k // 32))).repeat(32)
    a = np.empty((k // 512, 16))
    for p in range(k // 512):
        a[p, :8] = np.random.permutation(np.resize(levels, 8))
        for g in range(8):
            far = levels[np.abs(levels - a[p, g]) >= 10]
            a[p, g + 8] = far[np.random.randint(len(far))]
    return np.exp2(a.ravel()).repeat(32)


def f64(x):
    return np.asarray(x).astype(np.float64)


def striped(idx):
    return np.tile(np.asarray(idx).reshape(-1, 16).T, (8, 1)).astype(np.uint16)


def unstriped(offs):
    return offs[:16].T.reshape(-1).astype(np.int64)


E2M1 = np.array([0.0, 0.5, 1.0, 1.5, 2.0, 3.0, 4.0, 6.0, -0.0, -0.5, -1.0, -1.5, -2.0, -3.0, -4.0, -6.0])


def pack_weight(w, fmt):
    k, n = w.shape
    w = f64(np.asarray(w, np.float32).astype(ml_dtypes.bfloat16)).reshape(k // 32, 32, n)
    amax = np.abs(w).max(1)
    if fmt == "e4m3":
        byte = np.frexp(amax)[1] - 1 + 127 - 7
    else:
        mant, ex = np.frexp(amax / 6.0)
        byte = np.where(mant > 0.5, ex, ex - 1) + 127
    byte = np.clip(np.where(amax > 0, byte, 1), 1, 254)
    scaled = (w * np.exp2(127.0 - byte)[:, None, :]).reshape(k, n).astype(np.float32)
    by_word = np.ascontiguousarray(scaled.reshape(k // 512, 128, 4, n).transpose(0, 1, 3, 2))
    if fmt == "e4m3":
        words = by_word.astype(ml_dtypes.float8_e4m3fn).view(np.uint8)
    else:
        c = by_word.astype(ml_dtypes.float4_e2m1fn).view(np.uint8) & 0xF
        words = (c[..., 0::2] | (c[..., 1::2] << 4)).reshape(k // 512, 128, 2 * n)
    return np.ascontiguousarray(words), np.ascontiguousarray(byte.astype(np.uint8).reshape(k // 512, 16, n))


def unpack_weight(words, scales, fmt):
    g, _, n = scales.shape
    words = np.ascontiguousarray(words).reshape(g, 128, n, -1)
    if fmt == "e4m3":
        vals = words.view(ml_dtypes.float8_e4m3fn).astype(np.float64)
    else:
        nib = np.empty((g, 128, n, 4), np.uint8)
        nib[..., 0::2] = words & 0xF
        nib[..., 1::2] = words >> 4
        vals = E2M1[nib]
    vals = vals * np.repeat(np.exp2(scales.astype(np.float64) - 127.0), 8, axis=1)[..., None]
    return vals.transpose(0, 1, 3, 2).reshape(g * 512, n)


def sigmoid(v):
    return 1.0 / (1.0 + np.exp(-v))


K, T, Z, J, R, O, N, E = 512, 1024, 1024, 256, 512, 256, 256, 1024


def setup_inputs():
    n = np.random.standard_normal
    idx = np.random.permutation(T)[:J]
    idx2 = np.random.permutation(Z)[:J]
    idx3 = np.random.permutation(J)[:O]
    idx4 = np.random.permutation(O)[:O]
    idx5 = np.random.permutation(J)[:O]
    idx6 = np.random.permutation(T)[:O]
    idx7 = np.random.permutation(E)[:O]
    fk = mx_kscale(K)
    fr = mx_kscale(R)
    xtp = pack_weight(n((K, T)) / fk[:, None], "e2m1")
    xop = pack_weight(n((K, Z)) / fk[:, None], "e4m3")
    wp = pack_weight(n((K, R)) * 1 / np.sqrt(K) * fk[:, None] * fr, "e4m3")
    wbp = pack_weight(n((R, N)) * 1 / np.sqrt(R) / fr[:, None], "e2m1")
    wsp = pack_weight(n((K, N)) * 1 / np.sqrt(K) * fk[:, None], "e4m3")
    return {
        "xt_words": xtp[0],
        "xt_scales": xtp[1],
        "xo_words": xop[0],
        "xo_scales": xop[1],
        "w_words": wp[0],
        "w_scales": wp[1],
        "wb_words": wbp[0],
        "wb_scales": wbp[1],
        "ws_words": wsp[0],
        "ws_scales": wsp[1],
        "tz": (n((N, E))).astype(np.float32),
        "so": (np.random.uniform(0.6, 1.6, (N, 1))).astype(np.float32),
        "bo": (np.random.uniform(-1.0, 1.0, (N, 1))).astype(np.float32),
        "offs": striped(idx),
        "offs2": striped(idx2),
        "offs3": striped(idx3),
        "offs4": striped(idx4),
        "offs5": striped(idx5),
        "offs6": striped(idx6),
        "offs7": striped(idx7),
    }


def reference(xt_words, xt_scales, xo_words, xo_scales, w_words, w_scales, wb_words, wb_scales, ws_words, ws_scales, tz, so, bo, offs, offs2, offs3, offs4, offs5, offs6, offs7):
    idx = unstriped(offs)
    idx2 = unstriped(offs2)
    idx3 = unstriped(offs3)
    idx4 = unstriped(offs4)
    idx5 = unstriped(offs5)
    idx6 = unstriped(offs6)
    idx7 = unstriped(offs7)
    xtu = unpack_weight(xt_words, xt_scales, "e2m1")
    xou = unpack_weight(xo_words, xo_scales, "e4m3")
    wu = unpack_weight(w_words, w_scales, "e4m3")
    wbu = unpack_weight(wb_words, wb_scales, "e2m1")
    wsu = unpack_weight(ws_words, ws_scales, "e4m3")
    xtidxg = xtu[:, idx]
    a = wu.T @ xtidxg
    xoidx2g = xou[:, idx2]
    b = wu.T @ xoidx2g
    ca = a[:, idx3]
    hid = np.abs(ca[:, idx4] - b[:, idx5])
    hidq = mxq(hid, 0, "e5m2")
    xtidx6g = xtu[:, idx6]
    p = wbu.T @ hidq + wsu.T @ xtidx6g
    y = p * sigmoid(f64(tz)[:, idx7] * f64(so) + f64(bo))
    return y

@@ -1,0 +1,196 @@
+from contextlib import ExitStack
+
+import concourse.mybir as mybir
+
+F32 = mybir.dt.float32
+BF16 = mybir.dt.bfloat16
+I32 = mybir.dt.int32
+U32 = mybir.dt.uint32
+U16 = mybir.dt.uint16
+U8 = mybir.dt.uint8
+E4M3 = mybir.dt.float8_e4m3fn_x4
+E5M2 = mybir.dt.float8_e5m2_x4
+E2M1 = mybir.dt.float4_e2m1fn_x4
+ACT = mybir.ActivationFunctionType
+ALU = mybir.AluOpType
+
+P = 128
+PACK = 4
+TABLE = 1024
+J = 256
+R = 512
+N = 256
+HALF = 128
+FLOPS = 402653184
+
+
+def tile_list_secondhand_oneforboth_further_finalgate_kernel(
+    tc, xt_words, xt_scales, xo_words, xo_scales, w_words, w_scales, wb_words, wb_scales,
+    ws_words, ws_scales, tz, so, bo, offs, offs2, offs3, offs4, offs5, offs6, offs7, out
+):
+    nc = tc.nc
+    with ExitStack() as ctx:
+        pool = ctx.enter_context(tc.tile_pool(name="held", bufs=1))
+        psum = ctx.enter_context(tc.psum_pool(name="psum", bufs=1))
+
+        def tile(name, shape, dtype):
+            return pool.tile(shape, dtype, name=name, align_bytes=64)
+
+        def load_list(name, source):
+            held = tile(name, [P, J // 16], U16)
+            nc.sync.dma_start(held[:], source)
+            return held
+
+        def load_words(name, source, columns, dtype):
+            held = tile(name, [P, columns], dtype)
+            nc.sync.dma_start(out=held[:].bitcast(I32), in_=source.bitcast(I32))
+            return held
+
+        def load_scales(name, source, columns, queues):
+            held = tile(name, [P, columns], U8)
+            rows = source[0].bitcast(I32)
+            for q in range(4):
+                spread = rows[4 * q : 4 * q + 4, :].unsqueeze(0).broadcast_to([8, 4, columns // 4])
+                queues[q].dma_start(out=held[:].bitcast(I32)[32 * q : 32 * q + 32, :], in_=spread)
+            return held
+
+        def e4m3_rows(words):
+            return words[0].rearrange("p c t -> p (c t)")
+
+        idx = load_list("idx", offs)
+        xt_w = load_words("xt_w", xt_words[0], TABLE, U16)
+        xt_s = load_scales("xt_s", xt_scales, TABLE, [nc.scalar] * 4)
+        w_w = load_words("w_w", e4m3_rows(w_words), R, U32)
+        idx6 = load_list("idx6", offs6)
+        w_s = load_scales("w_s", w_scales, R, [nc.sync] * 4)
+        idx2 = load_list("idx2", offs2)
+        xo_w = load_words("xo_w", e4m3_rows(xo_words), TABLE, U32)
+        xo_s = load_scales("xo_s", xo_scales, TABLE, [nc.sync, nc.sync, nc.gpsimd, nc.gpsimd])
+        slope = tile("slope", [P, 2], F32)
+        offset = tile("offset", [P, 2], F32)
+        with nc.allow_non_contiguous_dma(reason="one value a partition"):
+            nc.gpsimd.dma_start(out=slope[:], in_=so.rearrange("(h p) o -> p (h o)", p=P))
+            nc.gpsimd.dma_start(out=offset[:], in_=bo.rearrange("(h p) o -> p (h o)", p=P))
+        idx3 = load_list("idx3", offs3)
+        idx5 = load_list("idx5", offs5)
+        idx4 = load_list("idx4", offs4)
+        idx7 = load_list("idx7", offs7)
+        tz_rows = [tile("tz_rows%d" % h, [P, TABLE], F32) for h in range(2)]
+        for h in range(2):
+            nc.sync.dma_start(out=tz_rows[h][:], in_=tz[h * P : (h + 1) * P, :])
+        ws_w = load_words("ws_w", e4m3_rows(ws_words), N, U32)
+        wb_w = load_words("wb_w", wb_words[0], N, U16)
+        ws_s = load_scales("ws_s", ws_scales, N, [nc.sync] * 4)
+        wb_s = load_scales("wb_s", wb_scales, N, [nc.sync] * 4)
+
+        def gather_packed(name, window, offsets, dtype):
+            picked = tile(name, [P, J], dtype)
+            nc.vector.tensor_copy(picked[:], window[:].indirect(offsets[:]))
+            return picked
+
+        def places(u):
+            return slice(u * HALF, (u + 1) * HALF)
+
+        def entries(u):
+            return slice(u * HALF // 16, (u + 1) * HALF // 16)
+
+        def on_scalar(dst, src):
+            nc.scalar.activation(out=dst, in_=src, func=ACT.Copy)
+
+        def on_vector(dst, src):
+            nc.vector.tensor_copy(out=dst, in_=src)
+
+        tok_w = gather_packed("tok_w", xt_w, idx, U16)
+        tok_s = gather_packed("tok_s", xt_s, idx, U8)
+        wt_w = tile("wt_w", [P, PACK, P], U32)
+        nc.vector.tensor_copy(
+            out=wt_w[:].bitcast(I32).rearrange("p t m -> p m t"),
+            in_=w_w[:].bitcast(I32).rearrange("p (m t) -> p m t", t=PACK),
+        )
+        short_w = gather_packed("short_w", xt_w, idx6, U16)
+        wt_s = tile("wt_s", [P, PACK, P], U8)
+        nc.vector.tensor_copy(
+            out=wt_s[:].rearrange("p t m -> p m t"),
+            in_=w_s[:].rearrange("p (m t) -> p m t", t=PACK),
+        )
+        note_w = gather_packed("note_w", xo_w, idx2, U32)
+        note_s = gather_packed("note_s", xo_s, idx2, U8)
+
+        def first_stage(name, moving_w, moving_s, fmt):
+            banks = [psum.tile([P, 2 * J], F32, name="%s_bank%d" % (name, i)) for i in range(2)]
+            for t in range(PACK):
+                nc.tensor.matmul_mx(
+                    out=banks[t // 2][:, (t % 2) * J : (t % 2 + 1) * J],
+                    lhsT=wt_w[:, t, :].bitcast(E4M3), lhsT_scale=wt_s[:, t, :],
+                    rhs=moving_w[:].bitcast(fmt), rhs_scale=moving_s[:],
+                    start=True, stop=True,
+                )
+            return banks
+
+        a_banks = first_stage("a", tok_w, tok_s, E2M1)
+        b_banks = first_stage("b", note_w, note_s, E4M3)
+
+        a_pair = [tile("a_pair%d" % i, [P, 2 * J], F32) for i in range(2)]
+        b_pair = [tile("b_pair%d" % i, [P, 2 * J], F32) for i in range(2)]
+        ca = [tile("ca%d" % t, [P, J], F32) for t in range(PACK)]
+        for i, move in enumerate((on_scalar, on_vector)):
+            move(a_pair[i][:], a_banks[i][:])
+            move(ca[2 * i][:], a_pair[i][:].indirect(idx3[:]))
+            for u in range(2):
+                move(ca[2 * i + 1][:, places(u)], a_pair[i][:, J : 2 * J].indirect(idx3[:, entries(u)]))
+        on_scalar(b_pair[0][:], b_banks[0][:])
+        on_vector(b_pair[1][:], b_banks[1][:])
+        short_s = gather_packed("short_s", xt_s, idx6, U8)
+
+        gates = tile("gates", [P, 2, J], F32)
+
+        def gate(h):
+            nc.scalar.activation(
+                out=gates[:, h, :], in_=tz_rows[h][:].indirect(idx7[:]), func=ACT.Sigmoid,
+                bias=offset[:, h : h + 1], scale=slope[:, h : h + 1],
+            )
+
+        out_rows = out.rearrange("(h p) o -> p h o", p=P)
+        sums = [psum.tile([P, 2, HALF], F32, name="sums%d" % u) for u in range(2)]
+        picked = [tile("picked%d" % u, [P, PACK, HALF], F32) for u in range(2)]
+        diff = [tile("diff%d" % u, [P, PACK, HALF], F32) for u in range(2)]
+        hid = [tile("hid%d" % u, [P, HALF, PACK], BF16) for u in range(2)]
+        hid_w = [tile("hid_w%d" % u, [P, HALF], U32) for u in range(2)]
+        hid_s = [tile("hid_s%d" % u, [P, HALF], U8) for u in range(2)]
+        y = [tile("y%d" % u, [P, 2, HALF], F32) for u in range(2)]
+
+        for u in range(2):
+            for h in range(2):
+                nc.tensor.matmul_mx(
+                    out=sums[u][:, h, :],
+                    lhsT=ws_w[:, h * P : (h + 1) * P].bitcast(E4M3), lhsT_scale=ws_s[:, h * P : (h + 1) * P],
+                    rhs=short_w[:, places(u)].bitcast(E2M1), rhs_scale=short_s[:, places(u)],
+                    start=(h == 0), stop=False,
+                )
+        for u in range(2):
+            for t in range(PACK):
+                b_plane = b_pair[t // 2][:, (t % 2) * J : (t % 2 + 1) * J]
+                on_scalar(picked[u][:, t, :], b_plane.indirect(idx5[:, entries(u)]))
+                nc.vector.tensor_tensor(
+                    diff[u][:, t, :], ca[t][:].indirect(idx4[:, entries(u)]), picked[u][:, t, :], ALU.subtract
+                )
+        gate(0)
+        gate(1)
+        for u in range(2):
+            nc.scalar.activation(
+                out=hid[u][:].rearrange("p (c i) t -> p c t i", i=4),
+                in_=diff[u][:].rearrange("p t (c i) -> p c t i", i=4),
+                func=ACT.Abs,
+            )
+            nc.vector.quantize_mx(
+                out=hid_w[u][:].bitcast(E5M2), scales=hid_s[u][:], in_=hid[u][:].rearrange("p c t -> p (c t)")
+            )
+            for h in range(2):
+                nc.tensor.matmul_mx(
+                    out=sums[u][:, h, :],
+                    lhsT=wb_w[:, h * P : (h + 1) * P].bitcast(E2M1), lhsT_scale=wb_s[:, h * P : (h + 1) * P],
+                    rhs=hid_w[u][:].bitcast(E5M2), rhs_scale=hid_s[u][:],
+                    start=False, stop=(h == 1),
+                )
+            nc.vector.tensor_tensor(y[u][:], sums[u][:], gates[:, :, places(u)], ALU.mult)
+            nc.sync.dma_start(out=out_rows[:, :, places(u)], in_=y[u][:])

@@ -46,42 +46,42 @@ def tile_list_secondhand_oneforboth_further_finalgate_kernel(
             nc.sync.dma_start(out=held[:].bitcast(I32), in_=source.bitcast(I32))
             return held
 
-        def load_scales(name, source, columns, queues):
+        def load_scales(name, source, columns, queue):
             held = tile(name, [P, columns], U8)
             rows = source[0].bitcast(I32)
             for q in range(4):
                 spread = rows[4 * q : 4 * q + 4, :].unsqueeze(0).broadcast_to([8, 4, columns // 4])
-                queues[q].dma_start(out=held[:].bitcast(I32)[32 * q : 32 * q + 32, :], in_=spread)
+                queue.dma_start(out=held[:].bitcast(I32)[32 * q : 32 * q + 32, :], in_=spread)
             return held
 
         def e4m3_rows(words):
             return words[0].rearrange("p c t -> p (c t)")
 
+        xt_s = load_scales("xt_s", xt_scales, TABLE, nc.scalar)
         idx = load_list("idx", offs)
-        xt_w = load_words("xt_w", xt_words[0], TABLE, U16)
-        xt_s = load_scales("xt_s", xt_scales, TABLE, [nc.scalar] * 4)
-        w_w = load_words("w_w", e4m3_rows(w_words), R, U32)
         idx6 = load_list("idx6", offs6)
-        w_s = load_scales("w_s", w_scales, R, [nc.sync] * 4)
-        idx2 = load_list("idx2", offs2)
+        xt_w = load_words("xt_w", xt_words[0], TABLE, U16)
+        w_w = load_words("w_w", e4m3_rows(w_words), R, U32)
+        w_s = load_scales("w_s", w_scales, R, nc.sync)
         xo_w = load_words("xo_w", e4m3_rows(xo_words), TABLE, U32)
-        xo_s = load_scales("xo_s", xo_scales, TABLE, [nc.sync, nc.sync, nc.gpsimd, nc.gpsimd])
+        idx2 = load_list("idx2", offs2)
+        idx3 = load_list("idx3", offs3)
+        idx5 = load_list("idx5", offs5)
+        xo_s = load_scales("xo_s", xo_scales, TABLE, nc.sync)
+        idx4 = load_list("idx4", offs4)
+        idx7 = load_list("idx7", offs7)
         slope = tile("slope", [P, 2], F32)
         offset = tile("offset", [P, 2], F32)
         with nc.allow_non_contiguous_dma(reason="one value a partition"):
             nc.gpsimd.dma_start(out=slope[:], in_=so.rearrange("(h p) o -> p (h o)", p=P))
             nc.gpsimd.dma_start(out=offset[:], in_=bo.rearrange("(h p) o -> p (h o)", p=P))
-        idx3 = load_list("idx3", offs3)
-        idx5 = load_list("idx5", offs5)
-        idx4 = load_list("idx4", offs4)
-        idx7 = load_list("idx7", offs7)
         tz_rows = [tile("tz_rows%d" % h, [P, TABLE], F32) for h in range(2)]
         for h in range(2):
             nc.sync.dma_start(out=tz_rows[h][:], in_=tz[h * P : (h + 1) * P, :])
         ws_w = load_words("ws_w", e4m3_rows(ws_words), N, U32)
         wb_w = load_words("wb_w", wb_words[0], N, U16)
-        ws_s = load_scales("ws_s", ws_scales, N, [nc.sync] * 4)
-        wb_s = load_scales("wb_s", wb_scales, N, [nc.sync] * 4)
+        ws_s = load_scales("ws_s", ws_scales, N, nc.sync)
+        wb_s = load_scales("wb_s", wb_scales, N, nc.gpsimd)
 
         def gather_packed(name, window, offsets, dtype):
             picked = tile(name, [P, J], dtype)
@@ -107,14 +107,15 @@ def tile_list_secondhand_oneforboth_further_finalgate_kernel(
             out=wt_w[:].bitcast(I32).rearrange("p t m -> p m t"),
             in_=w_w[:].bitcast(I32).rearrange("p (m t) -> p m t", t=PACK),
         )
-        short_w = gather_packed("short_w", xt_w, idx6, U16)
         wt_s = tile("wt_s", [P, PACK, P], U8)
         nc.vector.tensor_copy(
             out=wt_s[:].rearrange("p t m -> p m t"),
             in_=w_s[:].rearrange("p (m t) -> p m t", t=PACK),
         )
+        short_w = gather_packed("w_s", xt_w, idx6, U16)
+        short_s = gather_packed("xt_w", xt_s, idx6, U8)
         note_w = gather_packed("note_w", xo_w, idx2, U32)
-        note_s = gather_packed("note_s", xo_s, idx2, U8)
+        note_s = gather_packed("xo_w", xo_s, idx2, U8)
 
         def first_stage(name, moving_w, moving_s, fmt):
             banks = [psum.tile([P, 2 * J], F32, name="%s_bank%d" % (name, i)) for i in range(2)]
@@ -130,31 +131,22 @@ def tile_list_secondhand_oneforboth_further_finalgate_kernel(
         a_banks = first_stage("a", tok_w, tok_s, E2M1)
         b_banks = first_stage("b", note_w, note_s, E4M3)
 
-        a_pair = [tile("a_pair%d" % i, [P, 2 * J], F32) for i in range(2)]
+        a_pair = [tile(name, [P, 2 * J], F32) for name in ("a_pair0", "xo_s")]
         b_pair = [tile("b_pair%d" % i, [P, 2 * J], F32) for i in range(2)]
         ca = [tile("ca%d" % t, [P, J], F32) for t in range(PACK)]
         for i, move in enumerate((on_scalar, on_vector)):
             move(a_pair[i][:], a_banks[i][:])
-            move(ca[2 * i][:], a_pair[i][:].indirect(idx3[:]))
+            on_scalar(ca[2 * i][:], a_pair[i][:].indirect(idx3[:]))
             for u in range(2):
-                move(ca[2 * i + 1][:, places(u)], a_pair[i][:, J : 2 * J].indirect(idx3[:, entries(u)]))
-        on_scalar(b_pair[0][:], b_banks[0][:])
-        on_vector(b_pair[1][:], b_banks[1][:])
-        short_s = gather_packed("short_s", xt_s, idx6, U8)
-
-        gates = tile("gates", [P, 2, J], F32)
-
-        def gate(h):
-            nc.scalar.activation(
-                out=gates[:, h, :], in_=tz_rows[h][:].indirect(idx7[:]), func=ACT.Sigmoid,
-                bias=offset[:, h : h + 1], scale=slope[:, h : h + 1],
-            )
+                on_scalar(ca[2 * i + 1][:, places(u)], a_pair[i][:, J : 2 * J].indirect(idx3[:, entries(u)]))
+        for i in range(2):
+            on_vector(b_pair[i][:], b_banks[i][:])
 
         out_rows = out.rearrange("(h p) o -> p h o", p=P)
         sums = [psum.tile([P, 2, HALF], F32, name="sums%d" % u) for u in range(2)]
         picked = [tile("picked%d" % u, [P, PACK, HALF], F32) for u in range(2)]
         diff = [tile("diff%d" % u, [P, PACK, HALF], F32) for u in range(2)]
-        hid = [tile("hid%d" % u, [P, HALF, PACK], BF16) for u in range(2)]
+        hid = [tile(name, [P, HALF, PACK], BF16) for name in ("b_pair1", "hid1")]
         hid_w = [tile("hid_w%d" % u, [P, HALF], U32) for u in range(2)]
         hid_s = [tile("hid_s%d" % u, [P, HALF], U8) for u in range(2)]
         y = [tile("y%d" % u, [P, 2, HALF], F32) for u in range(2)]
@@ -171,17 +163,20 @@ def tile_list_secondhand_oneforboth_further_finalgate_kernel(
             for t in range(PACK):
                 b_plane = b_pair[t // 2][:, (t % 2) * J : (t % 2 + 1) * J]
                 on_scalar(picked[u][:, t, :], b_plane.indirect(idx5[:, entries(u)]))
+            for t in range(PACK):
                 nc.vector.tensor_tensor(
                     diff[u][:, t, :], ca[t][:].indirect(idx4[:, entries(u)]), picked[u][:, t, :], ALU.subtract
                 )
-        gate(0)
-        gate(1)
-        for u in range(2):
+        woven = [diff[u][:].rearrange("p t c -> p c t") for u in range(2)]
+        nc.scalar.activation(out=hid[0][:], in_=woven[0], func=ACT.Abs)
+        nc.vector.scalar_tensor_tensor(hid[1][:], woven[1], -1.0, woven[1], ALU.mult, ALU.max)
+        gates = tile("diff0", [P, 2, J], F32)
+        for h in range(2):
             nc.scalar.activation(
-                out=hid[u][:].rearrange("p (c i) t -> p c t i", i=4),
-                in_=diff[u][:].rearrange("p t (c i) -> p c t i", i=4),
-                func=ACT.Abs,
+                out=gates[:, h, :], in_=tz_rows[h][:].indirect(idx7[:]), func=ACT.Sigmoid,
+                bias=offset[:, h : h + 1], scale=slope[:, h : h + 1],
             )
+        for u in range(2):
             nc.vector.quantize_mx(
                 out=hid_w[u][:].bitcast(E5M2), scales=hid_s[u][:], in_=hid[u][:].rearrange("p c t -> p (c t)")
             )
@@ -192,5 +187,6 @@ def tile_list_secondhand_oneforboth_further_finalgate_kernel(
                     rhs=hid_w[u][:].bitcast(E5M2), rhs_scale=hid_s[u][:],
                     start=False, stop=(h == 1),
                 )
+        for u in range(2):
             nc.vector.tensor_tensor(y[u][:], sums[u][:], gates[:, :, places(u)], ALU.mult)
             nc.sync.dma_start(out=out_rows[:, :, places(u)], in_=y[u][:])

@@ -100,6 +100,9 @@ def tile_list_secondhand_oneforboth_further_finalgate_kernel(
         def on_vector(dst, src):
             nc.vector.tensor_copy(out=dst, in_=src)
 
+        warm = tile("warm", [P, 2], F32)
+        nc.vector.memset(warm[:, 0:1], 0.0)
+        nc.scalar.activation(out=warm[:, 1:2], in_=warm[:, 0:1], func=ACT.Sigmoid)
         tok_w = gather_packed("tok_w", xt_w, idx, U16)
         tok_s = gather_packed("tok_s", xt_s, idx, U8)
         wt_w = tile("wt_w", [P, PACK, P], U32)

@@ -73,15 +73,15 @@ def tile_list_secondhand_oneforboth_further_finalgate_kernel(
         slope = tile("slope", [P, 2], F32)
         offset = tile("offset", [P, 2], F32)
         with nc.allow_non_contiguous_dma(reason="one value a partition"):
-            nc.gpsimd.dma_start(out=slope[:], in_=so.rearrange("(h p) o -> p (h o)", p=P))
-            nc.gpsimd.dma_start(out=offset[:], in_=bo.rearrange("(h p) o -> p (h o)", p=P))
+            nc.sync.dma_start(out=slope[:], in_=so.rearrange("(h p) o -> p (h o)", p=P))
+            nc.sync.dma_start(out=offset[:], in_=bo.rearrange("(h p) o -> p (h o)", p=P))
         tz_rows = [tile("tz_rows%d" % h, [P, TABLE], F32) for h in range(2)]
         for h in range(2):
             nc.sync.dma_start(out=tz_rows[h][:], in_=tz[h * P : (h + 1) * P, :])
         ws_w = load_words("ws_w", e4m3_rows(ws_words), N, U32)
         wb_w = load_words("wb_w", wb_words[0], N, U16)
         ws_s = load_scales("ws_s", ws_scales, N, nc.sync)
-        wb_s = load_scales("wb_s", wb_scales, N, nc.gpsimd)
+        wb_s = load_scales("wb_s", wb_scales, N, nc.sync)
 
         def gather_packed(name, window, offsets, dtype):
             picked = tile(name, [P, J], dtype)
@@ -116,9 +116,9 @@ def tile_list_secondhand_oneforboth_further_finalgate_kernel(
             in_=w_s[:].rearrange("p (m t) -> p m t", t=PACK),
         )
         short_w = gather_packed("w_s", xt_w, idx6, U16)
-        short_s = gather_packed("xt_w", xt_s, idx6, U8)
         note_w = gather_packed("note_w", xo_w, idx2, U32)
-        note_s = gather_packed("xo_w", xo_s, idx2, U8)
+        note_s = gather_packed("note_s", xo_s, idx2, U8)
+        short_s = gather_packed("xo_s", xt_s, idx6, U8)
 
         def first_stage(name, moving_w, moving_s, fmt):
             banks = [psum.tile([P, 2 * J], F32, name="%s_bank%d" % (name, i)) for i in range(2)]
@@ -134,7 +134,7 @@ def tile_list_secondhand_oneforboth_further_finalgate_kernel(
         a_banks = first_stage("a", tok_w, tok_s, E2M1)
         b_banks = first_stage("b", note_w, note_s, E4M3)
 
-        a_pair = [tile(name, [P, 2 * J], F32) for name in ("a_pair0", "xo_s")]
+        a_pair = [tile(name, [P, 2 * J], F32) for name in ("a_pair0", "xo_w")]
         b_pair = [tile("b_pair%d" % i, [P, 2 * J], F32) for i in range(2)]
         ca = [tile("ca%d" % t, [P, J], F32) for t in range(PACK)]
         for i, move in enumerate((on_scalar, on_vector)):

from contextlib import ExitStack

import concourse.mybir as mybir

F32 = mybir.dt.float32
BF16 = mybir.dt.bfloat16
I32 = mybir.dt.int32
U32 = mybir.dt.uint32
U16 = mybir.dt.uint16
U8 = mybir.dt.uint8
E4M3 = mybir.dt.float8_e4m3fn_x4
E5M2 = mybir.dt.float8_e5m2_x4
E2M1 = mybir.dt.float4_e2m1fn_x4
ACT = mybir.ActivationFunctionType
ALU = mybir.AluOpType

P = 128
PACK = 4
TABLE = 1024
J = 256
R = 512
N = 256
HALF = 128
FLOPS = 402653184


def tile_list_secondhand_oneforboth_further_finalgate_kernel(
    tc, xt_words, xt_scales, xo_words, xo_scales, w_words, w_scales, wb_words, wb_scales,
    ws_words, ws_scales, tz, so, bo, offs, offs2, offs3, offs4, offs5, offs6, offs7, out
):
    nc = tc.nc
    with ExitStack() as ctx:
        pool = ctx.enter_context(tc.tile_pool(name="held", bufs=1))
        psum = ctx.enter_context(tc.psum_pool(name="psum", bufs=1))

        def tile(name, shape, dtype):
            return pool.tile(shape, dtype, name=name, align_bytes=64)

        def load_list(name, source):
            held = tile(name, [P, J // 16], U16)
            nc.sync.dma_start(held[:], source)
            return held

        def load_words(name, source, columns, dtype):
            held = tile(name, [P, columns], dtype)
            nc.sync.dma_start(out=held[:].bitcast(I32), in_=source.bitcast(I32))
            return held

        def load_scales(name, source, columns, queue):
            held = tile(name, [P, columns], U8)
            rows = source[0].bitcast(I32)
            for q in range(4):
                spread = rows[4 * q : 4 * q + 4, :].unsqueeze(0).broadcast_to([8, 4, columns // 4])
                queue.dma_start(out=held[:].bitcast(I32)[32 * q : 32 * q + 32, :], in_=spread)
            return held

        def e4m3_rows(words):
            return words[0].rearrange("p c t -> p (c t)")

        xt_s = load_scales("xt_s", xt_scales, TABLE, nc.scalar)
        idx = load_list("idx", offs)
        idx6 = load_list("idx6", offs6)
        xt_w = load_words("xt_w", xt_words[0], TABLE, U16)
        w_w = load_words("w_w", e4m3_rows(w_words), R, U32)
        w_s = load_scales("w_s", w_scales, R, nc.sync)
        xo_w = load_words("xo_w", e4m3_rows(xo_words), TABLE, U32)
        idx2 = load_list("idx2", offs2)
        idx3 = load_list("idx3", offs3)
        idx5 = load_list("idx5", offs5)
        xo_s = load_scales("xo_s", xo_scales, TABLE, nc.sync)
        idx4 = load_list("idx4", offs4)
        idx7 = load_list("idx7", offs7)
        slope = tile("slope", [P, 2], F32)
        offset = tile("offset", [P, 2], F32)
        with nc.allow_non_contiguous_dma(reason="one value a partition"):
            nc.sync.dma_start(out=slope[:], in_=so.rearrange("(h p) o -> p (h o)", p=P))
            nc.sync.dma_start(out=offset[:], in_=bo.rearrange("(h p) o -> p (h o)", p=P))
        tz_rows = [tile("tz_rows%d" % h, [P, TABLE], F32) for h in range(2)]
        for h in range(2):
            nc.sync.dma_start(out=tz_rows[h][:], in_=tz[h * P : (h + 1) * P, :])
        ws_w = load_words("ws_w", e4m3_rows(ws_words), N, U32)
        wb_w = load_words("wb_w", wb_words[0], N, U16)
        ws_s = load_scales("ws_s", ws_scales, N, nc.sync)
        wb_s = load_scales("wb_s", wb_scales, N, nc.sync)

        def gather_packed(name, window, offsets, dtype):
            picked = tile(name, [P, J], dtype)
            nc.vector.tensor_copy(picked[:], window[:].indirect(offsets[:]))
            return picked

        def places(u):
            return slice(u * HALF, (u + 1) * HALF)

        def entries(u):
            return slice(u * HALF // 16, (u + 1) * HALF // 16)

        def on_scalar(dst, src):
            nc.scalar.activation(out=dst, in_=src, func=ACT.Copy)

        def on_vector(dst, src):
            nc.vector.tensor_copy(out=dst, in_=src)

        warm = tile("warm", [P, 2], F32)
        nc.vector.memset(warm[:, 0:1], 0.0)
        nc.scalar.activation(out=warm[:, 1:2], in_=warm[:, 0:1], func=ACT.Sigmoid)
        tok_w = gather_packed("tok_w", xt_w, idx, U16)
        tok_s = gather_packed("tok_s", xt_s, idx, U8)
        wt_w = tile("wt_w", [P, PACK, P], U32)
        nc.vector.tensor_copy(
            out=wt_w[:].bitcast(I32).rearrange("p t m -> p m t"),
            in_=w_w[:].bitcast(I32).rearrange("p (m t) -> p m t", t=PACK),
        )
        wt_s = tile("wt_s", [P, PACK, P], U8)
        nc.vector.tensor_copy(
            out=wt_s[:].rearrange("p t m -> p m t"),
            in_=w_s[:].rearrange("p (m t) -> p m t", t=PACK),
        )
        short_w = gather_packed("w_s", xt_w, idx6, U16)
        note_w = gather_packed("note_w", xo_w, idx2, U32)
        note_s = gather_packed("note_s", xo_s, idx2, U8)
        short_s = gather_packed("xo_s", xt_s, idx6, U8)

        def first_stage(name, moving_w, moving_s, fmt):
            banks = [psum.tile([P, 2 * J], F32, name="%s_bank%d" % (name, i)) for i in range(2)]
            for t in range(PACK):
                nc.tensor.matmul_mx(
                    out=banks[t // 2][:, (t % 2) * J : (t % 2 + 1) * J],
                    lhsT=wt_w[:, t, :].bitcast(E4M3), lhsT_scale=wt_s[:, t, :],
                    rhs=moving_w[:].bitcast(fmt), rhs_scale=moving_s[:],
                    start=True, stop=True,
                )
            return banks

        a_banks = first_stage("a", tok_w, tok_s, E2M1)
        b_banks = first_stage("b", note_w, note_s, E4M3)

        a_pair = [tile(name, [P, 2 * J], F32) for name in ("a_pair0", "xo_w")]
        b_pair = [tile("b_pair%d" % i, [P, 2 * J], F32) for i in range(2)]
        ca = [tile("ca%d" % t, [P, J], F32) for t in range(PACK)]
        for i, move in enumerate((on_scalar, on_vector)):
            move(a_pair[i][:], a_banks[i][:])
            on_scalar(ca[2 * i][:], a_pair[i][:].indirect(idx3[:]))
            for u in range(2):
                on_scalar(ca[2 * i + 1][:, places(u)], a_pair[i][:, J : 2 * J].indirect(idx3[:, entries(u)]))
        for i in range(2):
            on_vector(b_pair[i][:], b_banks[i][:])

        out_rows = out.rearrange("(h p) o -> p h o", p=P)
        sums = [psum.tile([P, 2, HALF], F32, name="sums%d" % u) for u in range(2)]
        picked = [tile("picked%d" % u, [P, PACK, HALF], F32) for u in range(2)]
        diff = [tile("diff%d" % u, [P, PACK, HALF], F32) for u in range(2)]
        hid = [tile(name, [P, HALF, PACK], BF16) for name in ("b_pair1", "hid1")]
        hid_w = [tile("hid_w%d" % u, [P, HALF], U32) for u in range(2)]
        hid_s = [tile("hid_s%d" % u, [P, HALF], U8) for u in range(2)]
        y = [tile("y%d" % u, [P, 2, HALF], F32) for u in range(2)]

        for u in range(2):
            for h in range(2):
                nc.tensor.matmul_mx(
                    out=sums[u][:, h, :],
                    lhsT=ws_w[:, h * P : (h + 1) * P].bitcast(E4M3), lhsT_scale=ws_s[:, h * P : (h + 1) * P],
                    rhs=short_w[:, places(u)].bitcast(E2M1), rhs_scale=short_s[:, places(u)],
                    start=(h == 0), stop=False,
                )
        for u in range(2):
            for t in range(PACK):
                b_plane = b_pair[t // 2][:, (t % 2) * J : (t % 2 + 1) * J]
                on_scalar(picked[u][:, t, :], b_plane.indirect(idx5[:, entries(u)]))
            for t in range(PACK):
                nc.vector.tensor_tensor(
                    diff[u][:, t, :], ca[t][:].indirect(idx4[:, entries(u)]), picked[u][:, t, :], ALU.subtract
                )
        woven = [diff[u][:].rearrange("p t c -> p c t") for u in range(2)]
        nc.scalar.activation(out=hid[0][:], in_=woven[0], func=ACT.Abs)
        nc.vector.scalar_tensor_tensor(hid[1][:], woven[1], -1.0, woven[1], ALU.mult, ALU.max)
        gates = tile("diff0", [P, 2, J], F32)
        for h in range(2):
            nc.scalar.activation(
                out=gates[:, h, :], in_=tz_rows[h][:].indirect(idx7[:]), func=ACT.Sigmoid,
                bias=offset[:, h : h + 1], scale=slope[:, h : h + 1],
            )
        for u in range(2):
            nc.vector.quantize_mx(
                out=hid_w[u][:].bitcast(E5M2), scales=hid_s[u][:], in_=hid[u][:].rearrange("p c t -> p (c t)")
            )
            for h in range(2):
                nc.tensor.matmul_mx(
                    out=sums[u][:, h, :],
                    lhsT=wb_w[:, h * P : (h + 1) * P].bitcast(E2M1), lhsT_scale=wb_s[:, h * P : (h + 1) * P],
                    rhs=hid_w[u][:].bitcast(E5M2), rhs_scale=hid_s[u][:],
                    start=False, stop=(h == 1),
                )
        for u in range(2):
            nc.vector.tensor_tensor(y[u][:], sums[u][:], gates[:, :, places(u)], ALU.mult)
            nc.sync.dma_start(out=out_rows[:, :, places(u)], in_=y[u][:])
